import numpy as np
import ml_dtypes


def mxq(x, axis, fmt="e4m3"):
    dtype, down = {"e4m3": (ml_dtypes.float8_e4m3fn, 7), "e5m2": (ml_dtypes.float8_e5m2, 14)}[fmt]
    v = np.moveaxis(np.asarray(x, np.float32).astype(ml_dtypes.bfloat16).astype(np.float64), axis, -1)
    blocks = v.reshape(v.shape[:-1] + (-1, 32))
    amax = np.abs(blocks).max(-1, keepdims=True)
    byte = np.maximum(np.where(amax > 0, np.frexp(amax)[1] - 1 + 127, 0) - down, 1)
    scale = np.exp2(byte - 127.0)
    codes = (blocks / scale).astype(np.float32).astype(dtype).astype(np.float64)
    return np.moveaxis((codes * scale).reshape(v.shape), -1, axis)


WIDE = False


def mx_kscale(k):
    if not WIDE:
        return np.ones(k)
    levels = np.array([10, -10, 5, -5, 0])
    if k % 512:
        return np.exp2(np.random.permutation(np.resize(levels, k // 32))).repeat(32)
    a = np.empty((k // 512, 16))
    for p in range(k // 512):
        a[p, :8] = np.random.permutation(np.resize(levels, 8))
        for g in range(8):
            far = levels[np.abs(levels - a[p, g]) >= 10]
            a[p, g + 8] = far[np.random.randint(len(far))]
    return np.exp2(a.ravel()).repeat(32)


def f64(x):
    return np.asarray(x).astype(np.float64)


def striped(idx):
    return np.tile(idx.reshape(-1, 16).T, (8, 1)).astype(np.uint16)


def unstriped(offs):
    return offs[:16].T.reshape(-1).astype(np.int64)


def striped8(idx):
    return np.concatenate([x.reshape(-1, 16).T for x in idx]).astype(np.uint16)


def runs(offs, k):
    lists = np.stack([offs[16 * r : 16 * r + 16].T.reshape(-1) for r in range(8)]).astype(np.int64)
    return lists[np.arange(k) % 512 // 64]


def pack_weight(w):
    k, n = w.shape
    w = f64(np.asarray(w, np.float32).astype(ml_dtypes.bfloat16)).reshape(k // 32, 32, n)
    amax = np.abs(w).max(1)
    byte = np.clip(np.where(amax > 0, np.frexp(amax)[1] - 1 + 127 - 7, 1), 1, 254)
    scaled = (w * np.exp2(127.0 - byte)[:, None, :]).reshape(k, n).astype(np.float32)
    words = np.ascontiguousarray(scaled.reshape(k // 512, 128, 4, n).transpose(0, 1, 3, 2)).astype(ml_dtypes.float8_e4m3fn).view(np.uint8)
    return words, np.ascontiguousarray(byte.astype(np.uint8).reshape(k // 512, 16, n))


def unpack_weight(words, scales):
    g, p, n, _ = words.shape
    vals = np.ascontiguousarray(words).view(ml_dtypes.float8_e4m3fn).astype(np.float64) * np.repeat(np.exp2(scales.astype(np.float64) - 127.0), 8, axis=1)[..., None]
    return vals.transpose(0, 1, 3, 2).reshape(g * 512, n)


def sigmoid(v):
    return 1.0 / (1.0 + np.exp(-np.maximum(v, -700.0)))

def planes(y):
    n, m = y.shape
    v = y.astype(np.float32).astype(ml_dtypes.bfloat16).astype(np.float64).reshape(n // 32, 32, m)
    top = np.abs(v).max(1)
    byte = np.clip(np.where(top > 0, np.frexp(top)[1] - 1 + 127 - 7, 1), 1, 254)
    codes = (v * np.exp2(127.0 - byte)[:, None, :]).reshape(n, m).astype(np.float32).astype(ml_dtypes.float8_e4m3fn).view(np.uint8)
    words = codes.reshape(n // 512, 128, 4, m).transpose(0, 1, 3, 2)
    return np.ascontiguousarray(words), np.ascontiguousarray(byte.astype(np.uint8).reshape(n // 512, 16, m))


K, T, S, N, G, H = 512, 2048, 512, 512, 2048, 512


def setup_inputs():
    n = np.random.standard_normal
    s = mx_kscale(K)[:, None]
    u = mx_kscale(H)
    packed_xT = pack_weight(n((K, T)) * s)
    packed_dT = pack_weight(n((K, G)) / s)
    packed_w1 = pack_weight(n((H, N)) / np.sqrt(H) / u[:, None])
    packed_w2 = pack_weight(n((K, N)) / np.sqrt(K) / s)
    return {
        "x_words": packed_xT[0],
        "x_scales": packed_xT[1],
        "d_words": packed_dT[0],
        "d_scales": packed_dT[1],
        "gn": (np.random.uniform(0.5, 1.5, (H, 1)) * u[:, None]).astype(np.float32),
        "w1_words": packed_w1[0],
        "w1_scales": packed_w1[1],
        "w2_words": packed_w2[0],
        "w2_scales": packed_w2[1],
        "offs": striped(np.random.permutation(T)[:S]),
        "kidx": striped8(np.random.randint(0, G, (8, H))),
        "own": striped(np.random.permutation(T)[:S]),
    }


def reference(x_words, x_scales, d_words, d_scales, gn, w1_words, w1_scales, w2_words, w2_scales, offs, kidx, own):
    d_kidx = unpack_weight(d_words, d_scales)[np.arange(K)[:, None], runs(kidx, K)]
    xq = unpack_weight(x_words, x_scales)[:, unstriped(offs)]
    s = sigmoid(0.0625 * (d_kidx.T @ xq))
    z = f64(gn) * s
    h = unpack_weight(w1_words, w1_scales).T @ mxq(z, 0, "e4m3")
    x_own = unpack_weight(x_words, x_scales)[:, unstriped(own)]
    val = unpack_weight(w2_words, w2_scales).T @ x_own
    out_0 = h * val
    return (out_0,) + planes(out_0)

@@ -1,0 +1,206 @@
+from contextlib import ExitStack
+
+import concourse.mybir as mybir
+
+F32 = mybir.dt.float32
+BF16 = mybir.dt.bfloat16
+I32 = mybir.dt.int32
+U32 = mybir.dt.uint32
+U16 = mybir.dt.uint16
+U8 = mybir.dt.uint8
+FP8X4 = mybir.dt.float8_e4m3fn_x4
+MULT = mybir.AluOpType.mult
+SIGMOID = mybir.ActivationFunctionType.Sigmoid
+
+P = 128
+PACK = 4
+TABLE = 2048
+PICKED = 512
+CHUNK = 128
+CHUNKS = PICKED // CHUNK
+QUADS = 4
+FLOPS = 3 * 2 * 512 * 512 * 512
+
+
+def tile_picked_twostage_sigmoid_po_kernel(
+    tc, x_words, x_scales, d_words, d_scales, gn, w1_words, w1_scales, w2_words, w2_scales, offs, kidx, own,
+    out_0, out_1, out_2,
+):
+    nc = tc.nc
+
+    def words_of(dram):
+        return dram[0].rearrange("p n t -> p (n t)").bitcast(I32)
+
+    def deal_words(dst, src):
+        nc.vector.tensor_copy(
+            out=dst[:].rearrange("p (t c i) -> p c t i", t=PACK, i=4),
+            in_=src[:].rearrange("p (c i t) -> p c t i", t=PACK, i=4),
+        )
+
+    def deal_bytes(dst, src):
+        nc.vector.tensor_copy(
+            out=dst[:].rearrange("p (t c i) -> p c t i", t=PACK, i=16),
+            in_=src[:].rearrange("p (c i t) -> p c t i", t=PACK, i=16),
+        )
+
+    def mx(out, lhs_words, lhs_scales, rhs_words, rhs_scales):
+        nc.tensor.matmul_mx(
+            out=out, lhsT=lhs_words.bitcast(FP8X4), lhsT_scale=lhs_scales,
+            rhs=rhs_words.bitcast(FP8X4), rhs_scale=rhs_scales, start=True, stop=True,
+        )
+
+    with ExitStack() as ctx:
+        keep = ctx.enter_context(tc.tile_pool(name="keep", bufs=1))
+        shared = ctx.enter_context(tc.tile_pool(name="shared", bufs=1))
+        psum = ctx.enter_context(tc.psum_pool(name="psum", bufs=1))
+
+        def sb(name, shape, dtype, tag=""):
+            return keep.tile(shape, dtype, name=name, tag=tag, align_bytes=64)
+
+        def at(offset, name, shape, dtype):
+            return shared.tile(shape, dtype, name=name, offset=offset, align_bytes=64)
+
+        kidx_t = sb("kidx_t", [P, PICKED // 16], U16)
+        offs_t = sb("offs_t", [P, PICKED // 16], U16)
+        own_t = sb("own_t", [P, PICKED // 16], U16)
+        d_sc_tab = at(0, "d_sc_tab", [P, TABLE], U8)
+        x_sc_tab = sb("x_sc_tab", [P, TABLE], U8)
+        d_sc = sb("d_sc", [P, PICKED], U8)
+        gn_t = sb("gn_t", [P, PACK], F32, tag="d_table")
+
+        nc.vector.memset(d_sc_tab[:].bitcast(I32), 0)
+        nc.vector.memset(x_sc_tab[:].bitcast(I32), 0)
+        nc.vector.memset(d_sc[:].bitcast(I32), 0)
+
+        nc.sync.dma_start(gn_t[:], gn.rearrange("(p t) o -> p (t o)", t=PACK))
+        nc.sync.dma_start(kidx_t[:], kidx)
+        nc.sync.dma_start(offs_t[:], offs)
+        nc.sync.dma_start(own_t[:], own)
+        nc.sync.dma_start(d_sc_tab[:].bitcast(I32)[0:P:8, :], d_scales[0].bitcast(I32))
+        for q in range(QUADS):
+            nc.sync.dma_start(
+                x_sc_tab[:].bitcast(I32)[32 * q : 32 * q + 4, :], x_scales[0].bitcast(I32)[4 * q : 4 * q + 4, :]
+            )
+        gain = sb("gain", [P, CHUNK, PACK], F32)
+        nc.vector.tensor_copy(gain[:], gn_t[:].unsqueeze(1).to_broadcast([P, CHUNK, PACK]))
+        d_w_tab = sb("d_w_tab", [P, TABLE], U32, tag="d_table")
+        nc.sync.dma_start(d_w_tab[:].bitcast(I32), words_of(d_words))
+
+        d_sc_g = at(8192 + 4096 - 256, "d_sc_g", [P, PICKED], U8)
+        d_sc_dealt = sb("d_sc_dealt", [P, PICKED], U8)
+        nc.vector.tensor_copy(d_sc_g[:], d_sc_tab[:].indirect(kidx_t[:]))
+        x_w_tab = at(0, "x_w_tab", [P, TABLE], U32)
+        nc.sync.dma_start(x_w_tab[:].bitcast(I32), words_of(x_words))
+        deal_bytes(d_sc_dealt, d_sc_g)
+        for q in range(QUADS):
+            nc.sync.dma_start(
+                d_sc[:].bitcast(I32)[32 * q : 32 * q + 4, :], d_sc_dealt[:].bitcast(I32)[32 * q : 32 * q + 32 : 8, :]
+            )
+
+        w_raw = at(8192, "w_raw", [P, 2 * PICKED], U32)
+        w_sc_raw = at(8192 + 4096, "w_sc_raw", [P, PICKED], U8)
+        nc.gpsimd.memset(w_sc_raw[:].bitcast(I32), 0)
+        nc.sync.dma_start(w_raw[:].bitcast(I32)[:, 0:PICKED], words_of(w2_words))
+        for first, scales in ((4, w2_scales), (0, w1_scales)):
+            for q in range(QUADS):
+                nc.sync.dma_start(
+                    w_sc_raw[:].bitcast(I32)[32 * q + first : 32 * q + first + 4, :],
+                    scales[0].bitcast(I32)[4 * q : 4 * q + 4, :],
+                )
+        nc.sync.dma_start(w_raw[:].bitcast(I32)[:, PICKED : 2 * PICKED], words_of(w1_words))
+
+        xq_sc = sb("xq_sc", [P, PICKED], U8)
+        nc.vector.tensor_copy(xq_sc[:], x_sc_tab[:].indirect(offs_t[:]))
+        d_w_g = sb("d_w_g", [P, PICKED], U32)
+        d_w = sb("d_w", [P, PICKED], U32)
+        nc.vector.tensor_copy(d_w_g[:], d_w_tab[:].indirect(kidx_t[:]))
+        deal_words(d_w, d_w_g)
+        xq_w = sb("xq_w", [P, PICKED], U32)
+        nc.vector.tensor_copy(xq_w[:], x_w_tab[:].indirect(offs_t[:]))
+        xo_sc = sb("xo_sc", [P, PICKED], U8)
+        nc.vector.tensor_copy(xo_sc[:], x_sc_tab[:].indirect(own_t[:]))
+        xo_w = sb("xo_w", [P, PICKED], U32)
+        nc.vector.tensor_copy(xo_w[:], x_w_tab[:].indirect(own_t[:]))
+        w_w = at(0, "w_w", [P, 2 * PICKED], U32)
+        w_sc = at(4 * 2 * PICKED, "w_sc", [P, PICKED], U8)
+        w2_w, w1_w = w_w[:, 0:PICKED], w_w[:, PICKED : 2 * PICKED]
+        deal_words(w2_w, w_raw[:, 0:PICKED])
+
+        def cols(i):
+            return slice(i * CHUNK, (i + 1) * CHUNK)
+
+        s_sb = []
+        for c in range(CHUNKS):
+            bank = psum.tile([P, PACK, CHUNK], F32, name=f"score{c}", tag=f"a{c}")
+            for t in range(PACK):
+                mx(bank[:, t, :], d_w[:, cols(t)], d_sc[:, cols(t)], xq_w[:, cols(c)], xq_sc[:, cols(c)])
+            s = sb(f"s{c}", [P, CHUNK, PACK], F32)
+            nc.scalar.activation(s[:], bank[:].rearrange("p t n -> p n t"), SIGMOID, scale=0.0625)
+            s_sb.append(s)
+
+        z_bf, h_banks, y_bf = {}, {}, {}
+
+        def weigh(c):
+            z_bf[c] = sb(f"z{c}", [P, CHUNK, PACK], BF16)
+            nc.vector.tensor_tensor(z_bf[c][:], s_sb[c][:], gain[:], MULT)
+
+        weigh(0)
+        deal_bytes(w_sc, w_sc_raw)
+        deal_words(w1_w, w_raw[:, PICKED : 2 * PICKED])
+        val_sb = []
+        for c in range(CHUNKS):
+            bank = psum.tile([P, PACK, CHUNK], F32, name=f"val{c}", tag=f"b{c}")
+            for t in range(PACK):
+                mx(bank[:, t, :], w2_w[:, cols(t)], w_sc[4:P, cols(t)], xo_w[:, cols(c)], xo_sc[:, cols(c)])
+            v = sb(f"v{c}", [P, PACK, CHUNK], F32)
+            nc.scalar.copy(v[:], bank[:])
+            val_sb.append(v)
+
+        y_w = sb("y_w", [P, PICKED], U32)
+        y_sc = sb("y_sc", [P, PICKED], U8)
+        out_rows = out_0.rearrange("(p t) j -> p t j", t=PACK)
+
+        def second_product(c):
+            zw = sb(f"zw{c}", [P, CHUNK], U32)
+            zs = sb(f"zs{c}", [P, CHUNK], U8)
+            nc.vector.quantize_mx(zw[:].bitcast(FP8X4), zs[:], z_bf[c][:].rearrange("p n t -> p (n t)"))
+            h_banks[c] = psum.tile([P, PACK, CHUNK], F32, name=f"h{c}", tag=f"a{c}")
+            for t in range(PACK):
+                mx(h_banks[c][:, t, :], w1_w[:, cols(t)], w_sc[:, cols(t)], zw[:], zs[:])
+
+        def result(c):
+            y = sb(f"y{c}", [P, PACK, CHUNK], F32)
+            nc.vector.tensor_tensor(y[:], h_banks[c][:], val_sb[c][:], MULT)
+            nc.sync.dma_start(out_rows[:, :, cols(c)], y[:])
+            y_bf[c] = sb(f"yb{c}", [P, CHUNK, PACK], BF16)
+            nc.scalar.copy(y_bf[c][:], y[:].rearrange("p t n -> p n t"))
+
+        def planes(c):
+            nc.vector.quantize_mx(
+                y_w[:, cols(c)].bitcast(FP8X4), y_sc[:, cols(c)], y_bf[c][:].rearrange("p n t -> p (n t)")
+            )
+
+        weigh(1)
+        second_product(0)
+        weigh(2)
+        second_product(1)
+        result(0)
+        weigh(3)
+        second_product(2)
+        result(1)
+        second_product(3)
+        planes(0)
+        result(2)
+        planes(1)
+        result(3)
+        planes(2)
+        out_words = words_of(out_1)
+        last = (CHUNKS - 1) * CHUNK
+        nc.sync.dma_start(out_words[:, 0:last], y_w[:].bitcast(I32)[:, 0:last])
+        planes(3)
+        nc.sync.dma_start(out_words[:, last:PICKED], y_w[:].bitcast(I32)[:, last:PICKED])
+        for q in range(QUADS):
+            queue = nc.scalar if q % 2 else nc.sync
+            queue.dma_start(
+                out_2[0].bitcast(I32)[4 * q : 4 * q + 4, :], y_sc[:].bitcast(I32)[32 * q : 32 * q + 4, :]
+            )

@@ -51,22 +51,20 @@ def tile_picked_twostage_sigmoid_po_kernel(
 
     with ExitStack() as ctx:
         keep = ctx.enter_context(tc.tile_pool(name="keep", bufs=1))
-        shared = ctx.enter_context(tc.tile_pool(name="shared", bufs=1))
         psum = ctx.enter_context(tc.psum_pool(name="psum", bufs=1))
 
         def sb(name, shape, dtype, tag=""):
             return keep.tile(shape, dtype, name=name, tag=tag, align_bytes=64)
 
-        def at(offset, name, shape, dtype):
-            return shared.tile(shape, dtype, name=name, offset=offset, align_bytes=64)
-
         kidx_t = sb("kidx_t", [P, PICKED // 16], U16)
         offs_t = sb("offs_t", [P, PICKED // 16], U16)
         own_t = sb("own_t", [P, PICKED // 16], U16)
-        d_sc_tab = at(0, "d_sc_tab", [P, TABLE], U8)
+        d_sc_tab = sb("d_sc_tab", [P, TABLE], U8)
         x_sc_tab = sb("x_sc_tab", [P, TABLE], U8)
         d_sc = sb("d_sc", [P, PICKED], U8)
         gn_t = sb("gn_t", [P, PACK], F32, tag="d_table")
+        w1_raw = sb("w1_raw", [P, PICKED], U32)
+        w2_raw = sb("w2_raw", [P, PICKED], U32, tag="x_table")
 
         nc.vector.memset(d_sc_tab[:].bitcast(I32), 0)
         nc.vector.memset(x_sc_tab[:].bitcast(I32), 0)
@@ -76,6 +74,8 @@ def tile_picked_twostage_sigmoid_po_kernel(
         nc.sync.dma_start(kidx_t[:], kidx)
         nc.sync.dma_start(offs_t[:], offs)
         nc.sync.dma_start(own_t[:], own)
+        nc.sync.dma_start(w2_raw[:].bitcast(I32), words_of(w2_words))
+        nc.sync.dma_start(w1_raw[:].bitcast(I32), words_of(w1_words))
         nc.sync.dma_start(d_sc_tab[:].bitcast(I32)[0:P:8, :], d_scales[0].bitcast(I32))
         for q in range(QUADS):
             nc.sync.dma_start(
@@ -86,28 +86,29 @@ def tile_picked_twostage_sigmoid_po_kernel(
         d_w_tab = sb("d_w_tab", [P, TABLE], U32, tag="d_table")
         nc.sync.dma_start(d_w_tab[:].bitcast(I32), words_of(d_words))
 
-        d_sc_g = at(8192 + 4096 - 256, "d_sc_g", [P, PICKED], U8)
+        w2_w = sb("w2_w", [P, PICKED], U32)
+        w1_w = sb("w1_w", [P, PICKED], U32)
+        deal_words(w2_w, w2_raw)
+        x_w_tab = sb("x_w_tab", [P, TABLE], U32, tag="x_table")
+        nc.sync.dma_start(x_w_tab[:].bitcast(I32), words_of(x_words))
+        deal_words(w1_w, w1_raw)
+        d_sc_g = sb("d_sc_g", [P, PICKED], U8, tag="scale_stage")
         d_sc_dealt = sb("d_sc_dealt", [P, PICKED], U8)
         nc.vector.tensor_copy(d_sc_g[:], d_sc_tab[:].indirect(kidx_t[:]))
-        x_w_tab = at(0, "x_w_tab", [P, TABLE], U32)
-        nc.sync.dma_start(x_w_tab[:].bitcast(I32), words_of(x_words))
         deal_bytes(d_sc_dealt, d_sc_g)
         for q in range(QUADS):
             nc.sync.dma_start(
                 d_sc[:].bitcast(I32)[32 * q : 32 * q + 4, :], d_sc_dealt[:].bitcast(I32)[32 * q : 32 * q + 32 : 8, :]
             )
 
-        w_raw = at(8192, "w_raw", [P, 2 * PICKED], U32)
-        w_sc_raw = at(8192 + 4096, "w_sc_raw", [P, PICKED], U8)
+        w_sc_raw = sb("w_sc_raw", [P, PICKED], U8, tag="scale_stage")
         nc.gpsimd.memset(w_sc_raw[:].bitcast(I32), 0)
-        nc.sync.dma_start(w_raw[:].bitcast(I32)[:, 0:PICKED], words_of(w2_words))
         for first, scales in ((4, w2_scales), (0, w1_scales)):
             for q in range(QUADS):
                 nc.sync.dma_start(
                     w_sc_raw[:].bitcast(I32)[32 * q + first : 32 * q + first + 4, :],
                     scales[0].bitcast(I32)[4 * q : 4 * q + 4, :],
                 )
-        nc.sync.dma_start(w_raw[:].bitcast(I32)[:, PICKED : 2 * PICKED], words_of(w1_words))
 
         xq_sc = sb("xq_sc", [P, PICKED], U8)
         nc.vector.tensor_copy(xq_sc[:], x_sc_tab[:].indirect(offs_t[:]))
@@ -121,10 +122,7 @@ def tile_picked_twostage_sigmoid_po_kernel(
         nc.vector.tensor_copy(xo_sc[:], x_sc_tab[:].indirect(own_t[:]))
         xo_w = sb("xo_w", [P, PICKED], U32)
         nc.vector.tensor_copy(xo_w[:], x_w_tab[:].indirect(own_t[:]))
-        w_w = at(0, "w_w", [P, 2 * PICKED], U32)
-        w_sc = at(4 * 2 * PICKED, "w_sc", [P, PICKED], U8)
-        w2_w, w1_w = w_w[:, 0:PICKED], w_w[:, PICKED : 2 * PICKED]
-        deal_words(w2_w, w_raw[:, 0:PICKED])
+        w_sc = sb("w_sc", [P, PICKED], U8, tag="x_table")
 
         def cols(i):
             return slice(i * CHUNK, (i + 1) * CHUNK)
@@ -138,23 +136,25 @@ def tile_picked_twostage_sigmoid_po_kernel(
             nc.scalar.activation(s[:], bank[:].rearrange("p t n -> p n t"), SIGMOID, scale=0.0625)
             s_sb.append(s)
 
-        z_bf, h_banks, y_bf = {}, {}, {}
+        h_banks, y_bf = {}, {}
 
         def weigh(c):
-            z_bf[c] = sb(f"z{c}", [P, CHUNK, PACK], BF16)
-            nc.vector.tensor_tensor(z_bf[c][:], s_sb[c][:], gain[:], MULT)
+            nc.vector.tensor_tensor(
+                z_bf[:, c * PACK * CHUNK : (c + 1) * PACK * CHUNK],
+                s_sb[c][:].rearrange("p n t -> p (n t)"), gain[:].rearrange("p n t -> p (n t)"), MULT,
+            )
 
-        weigh(0)
         deal_bytes(w_sc, w_sc_raw)
-        deal_words(w1_w, w_raw[:, PICKED : 2 * PICKED])
-        val_sb = []
-        for c in range(CHUNKS):
+        z_bf = sb("z_bf", [P, PACK * PICKED], BF16, tag="scale_stage")
+        val_sb = {}
+
+        def projection(c):
             bank = psum.tile([P, PACK, CHUNK], F32, name=f"val{c}", tag=f"b{c}")
             for t in range(PACK):
                 mx(bank[:, t, :], w2_w[:, cols(t)], w_sc[4:P, cols(t)], xo_w[:, cols(c)], xo_sc[:, cols(c)])
             v = sb(f"v{c}", [P, PACK, CHUNK], F32)
             nc.scalar.copy(v[:], bank[:])
-            val_sb.append(v)
+            val_sb[c] = v
 
         y_w = sb("y_w", [P, PICKED], U32)
         y_sc = sb("y_sc", [P, PICKED], U8)
@@ -163,7 +163,7 @@ def tile_picked_twostage_sigmoid_po_kernel(
         def second_product(c):
             zw = sb(f"zw{c}", [P, CHUNK], U32)
             zs = sb(f"zs{c}", [P, CHUNK], U8)
-            nc.vector.quantize_mx(zw[:].bitcast(FP8X4), zs[:], z_bf[c][:].rearrange("p n t -> p (n t)"))
+            nc.vector.quantize_mx(zw[:].bitcast(FP8X4), zs[:], z_bf[:, c * PACK * CHUNK : (c + 1) * PACK * CHUNK])
             h_banks[c] = psum.tile([P, PACK, CHUNK], F32, name=f"h{c}", tag=f"a{c}")
             for t in range(PACK):
                 mx(h_banks[c][:, t, :], w1_w[:, cols(t)], w_sc[:, cols(t)], zw[:], zs[:])
@@ -180,10 +180,15 @@ def tile_picked_twostage_sigmoid_po_kernel(
                 y_w[:, cols(c)].bitcast(FP8X4), y_sc[:, cols(c)], y_bf[c][:].rearrange("p n t -> p (n t)")
             )
 
+        projection(0)
+        weigh(0)
+        projection(1)
         weigh(1)
         second_product(0)
+        projection(2)
         weigh(2)
         second_product(1)
+        projection(3)
         result(0)
         weigh(3)
         second_product(2)

@@ -92,17 +92,22 @@ def tile_picked_twostage_sigmoid_po_kernel(
         x_w_tab = sb("x_w_tab", [P, TABLE], U32, tag="x_table")
         nc.sync.dma_start(x_w_tab[:].bitcast(I32), words_of(x_words))
         deal_words(w1_w, w1_raw)
-        d_sc_g = sb("d_sc_g", [P, PICKED], U8, tag="scale_stage")
+        d_sc_g = sb("d_sc_g", [P, PICKED], U8)
         d_sc_dealt = sb("d_sc_dealt", [P, PICKED], U8)
         nc.vector.tensor_copy(d_sc_g[:], d_sc_tab[:].indirect(kidx_t[:]))
+        xq_sc = sb("xq_sc", [P, PICKED], U8)
+        nc.vector.tensor_copy(xq_sc[:], x_sc_tab[:].indirect(offs_t[:]))
         deal_bytes(d_sc_dealt, d_sc_g)
         for q in range(QUADS):
             nc.sync.dma_start(
                 d_sc[:].bitcast(I32)[32 * q : 32 * q + 4, :], d_sc_dealt[:].bitcast(I32)[32 * q : 32 * q + 32 : 8, :]
             )
 
-        w_sc_raw = sb("w_sc_raw", [P, PICKED], U8, tag="scale_stage")
-        nc.gpsimd.memset(w_sc_raw[:].bitcast(I32), 0)
+        d_w_g = sb("d_w_g", [P, PICKED], U32)
+        d_w = sb("d_w", [P, PICKED], U32)
+        nc.vector.tensor_copy(d_w_g[:], d_w_tab[:].indirect(kidx_t[:]))
+        w_sc_raw = sb("w_sc_raw", [P, PICKED], U8, tag="d_table")
+        nc.vector.memset(w_sc_raw[:].bitcast(I32), 0)
         for first, scales in ((4, w2_scales), (0, w1_scales)):
             for q in range(QUADS):
                 nc.sync.dma_start(
@@ -110,16 +115,12 @@ def tile_picked_twostage_sigmoid_po_kernel(
                     scales[0].bitcast(I32)[4 * q : 4 * q + 4, :],
                 )
 
-        xq_sc = sb("xq_sc", [P, PICKED], U8)
-        nc.vector.tensor_copy(xq_sc[:], x_sc_tab[:].indirect(offs_t[:]))
-        d_w_g = sb("d_w_g", [P, PICKED], U32)
-        d_w = sb("d_w", [P, PICKED], U32)
-        nc.vector.tensor_copy(d_w_g[:], d_w_tab[:].indirect(kidx_t[:]))
         deal_words(d_w, d_w_g)
-        xq_w = sb("xq_w", [P, PICKED], U32)
-        nc.vector.tensor_copy(xq_w[:], x_w_tab[:].indirect(offs_t[:]))
-        xo_sc = sb("xo_sc", [P, PICKED], U8)
-        nc.vector.tensor_copy(xo_sc[:], x_sc_tab[:].indirect(own_t[:]))
+        xq_w = []
+        for half in range(2):
+            xq_half = sb(f"xq_w{half}", [P, PICKED // 2], U32, tag=f"query{half}")
+            nc.vector.tensor_copy(xq_half[:], x_w_tab[:].indirect(offs_t[:, 16 * half : 16 * half + 16]))
+            xq_w.append(xq_half)
         xo_w = sb("xo_w", [P, PICKED], U32)
         nc.vector.tensor_copy(xo_w[:], x_w_tab[:].indirect(own_t[:]))
         w_sc = sb("w_sc", [P, PICKED], U8, tag="x_table")
@@ -131,11 +132,13 @@ def tile_picked_twostage_sigmoid_po_kernel(
         for c in range(CHUNKS):
             bank = psum.tile([P, PACK, CHUNK], F32, name=f"score{c}", tag=f"a{c}")
             for t in range(PACK):
-                mx(bank[:, t, :], d_w[:, cols(t)], d_sc[:, cols(t)], xq_w[:, cols(c)], xq_sc[:, cols(c)])
+                mx(bank[:, t, :], d_w[:, cols(t)], d_sc[:, cols(t)], xq_w[c // 2][:, cols(c % 2)], xq_sc[:, cols(c)])
             s = sb(f"s{c}", [P, CHUNK, PACK], F32)
             nc.scalar.activation(s[:], bank[:].rearrange("p t n -> p n t"), SIGMOID, scale=0.0625)
             s_sb.append(s)
 
+        xo_sc = sb("xo_sc", [P, PICKED], U8, tag="query0")
+        nc.vector.tensor_copy(xo_sc[:], x_sc_tab[:].indirect(own_t[:]))
         h_banks, y_bf = {}, {}
 
         def weigh(c):
@@ -145,7 +148,7 @@ def tile_picked_twostage_sigmoid_po_kernel(
             )
 
         deal_bytes(w_sc, w_sc_raw)
-        z_bf = sb("z_bf", [P, PACK * PICKED], BF16, tag="scale_stage")
+        z_bf = sb("z_bf", [P, PACK * PICKED], BF16, tag="d_table")
         val_sb = {}
 
         def projection(c):
@@ -170,15 +173,25 @@ def tile_picked_twostage_sigmoid_po_kernel(
 
         def result(c):
             y = sb(f"y{c}", [P, PACK, CHUNK], F32)
-            nc.vector.tensor_tensor(y[:], h_banks[c][:], val_sb[c][:], MULT)
-            nc.sync.dma_start(out_rows[:, :, cols(c)], y[:])
             y_bf[c] = sb(f"yb{c}", [P, CHUNK, PACK], BF16)
-            nc.scalar.copy(y_bf[c][:], y[:].rearrange("p t n -> p n t"))
+            parts = 2 if c == CHUNKS - 1 else 1
+            width = CHUNK // parts
+            for part in range(parts):
+                n = slice(part * width, (part + 1) * width)
+                nc.vector.tensor_tensor(y[:, :, n], h_banks[c][:, :, n], val_sb[c][:, :, n], MULT)
+                nc.scalar.copy(
+                    y_bf[c][:, n, :].rearrange("p (m i) t -> p m t i", i=4),
+                    y[:, :, n].rearrange("p t (m i) -> p m t i", i=4),
+                )
+            nc.sync.dma_start(out_rows[:, :, cols(c)], y[:])
 
         def planes(c):
             nc.vector.quantize_mx(
                 y_w[:, cols(c)].bitcast(FP8X4), y_sc[:, cols(c)], y_bf[c][:].rearrange("p n t -> p (n t)")
             )
+            if c % 2:
+                pair = slice((c - 1) * CHUNK, (c + 1) * CHUNK)
+                nc.sync.dma_start(words_of(out_1)[:, pair], y_w[:].bitcast(I32)[:, pair])
 
         projection(0)
         weigh(0)
@@ -199,13 +212,9 @@ def tile_picked_twostage_sigmoid_po_kernel(
         planes(1)
         result(3)
         planes(2)
-        out_words = words_of(out_1)
-        last = (CHUNKS - 1) * CHUNK
-        nc.sync.dma_start(out_words[:, 0:last], y_w[:].bitcast(I32)[:, 0:last])
         planes(3)
-        nc.sync.dma_start(out_words[:, last:PICKED], y_w[:].bitcast(I32)[:, last:PICKED])
         for q in range(QUADS):
-            queue = nc.scalar if q % 2 else nc.sync
+            queue = nc.sync if q == QUADS - 1 else nc.scalar
             queue.dma_start(
                 out_2[0].bitcast(I32)[4 * q : 4 * q + 4, :], y_sc[:].bitcast(I32)[32 * q : 32 * q + 4, :]
             )

@@ -1,6 +1,7 @@
 from contextlib import ExitStack
 
 import concourse.mybir as mybir
+from concourse.masks import make_identity
 
 F32 = mybir.dt.float32
 BF16 = mybir.dt.bfloat16
@@ -59,7 +60,7 @@ def tile_picked_twostage_sigmoid_po_kernel(
         kidx_t = sb("kidx_t", [P, PICKED // 16], U16)
         offs_t = sb("offs_t", [P, PICKED // 16], U16)
         own_t = sb("own_t", [P, PICKED // 16], U16)
-        d_sc_tab = sb("d_sc_tab", [P, TABLE], U8)
+        d_sc_tab = sb("d_sc_tab", [P, TABLE], U8, tag="scratch")
         x_sc_tab = sb("x_sc_tab", [P, TABLE], U8)
         d_sc = sb("d_sc", [P, PICKED], U8)
         gn_t = sb("gn_t", [P, PACK], F32, tag="d_table")
@@ -69,6 +70,9 @@ def tile_picked_twostage_sigmoid_po_kernel(
         nc.vector.memset(d_sc_tab[:].bitcast(I32), 0)
         nc.vector.memset(x_sc_tab[:].bitcast(I32), 0)
         nc.vector.memset(d_sc[:].bitcast(I32), 0)
+
+        identity = sb("identity", [P, P], F32)
+        make_identity(nc, identity[:])
 
         nc.sync.dma_start(gn_t[:], gn.rearrange("(p t) o -> p (t o)", t=PACK))
         nc.sync.dma_start(kidx_t[:], kidx)
@@ -93,20 +97,15 @@ def tile_picked_twostage_sigmoid_po_kernel(
         nc.sync.dma_start(x_w_tab[:].bitcast(I32), words_of(x_words))
         deal_words(w1_w, w1_raw)
         d_sc_g = sb("d_sc_g", [P, PICKED], U8)
-        d_sc_dealt = sb("d_sc_dealt", [P, PICKED], U8)
         nc.vector.tensor_copy(d_sc_g[:], d_sc_tab[:].indirect(kidx_t[:]))
-        xq_sc = sb("xq_sc", [P, PICKED], U8)
-        nc.vector.tensor_copy(xq_sc[:], x_sc_tab[:].indirect(offs_t[:]))
-        deal_bytes(d_sc_dealt, d_sc_g)
         for q in range(QUADS):
             nc.sync.dma_start(
-                d_sc[:].bitcast(I32)[32 * q : 32 * q + 4, :], d_sc_dealt[:].bitcast(I32)[32 * q : 32 * q + 32 : 8, :]
+                d_sc[:].bitcast(I32)[32 * q : 32 * q + 4, :], d_sc_g[:].bitcast(I32)[32 * q : 32 * q + 32 : 8, :]
             )
 
-        d_w_g = sb("d_w_g", [P, PICKED], U32)
-        d_w = sb("d_w", [P, PICKED], U32)
-        nc.vector.tensor_copy(d_w_g[:], d_w_tab[:].indirect(kidx_t[:]))
-        w_sc_raw = sb("w_sc_raw", [P, PICKED], U8, tag="d_table")
+        xq_sc = sb("xq_sc", [P, PICKED], U8)
+        nc.vector.tensor_copy(xq_sc[:], x_sc_tab[:].indirect(offs_t[:]))
+        w_sc_raw = sb("w_sc_raw", [P, PICKED], U8, tag="scratch")
         nc.vector.memset(w_sc_raw[:].bitcast(I32), 0)
         for first, scales in ((4, w2_scales), (0, w1_scales)):
             for q in range(QUADS):
@@ -115,10 +114,13 @@ def tile_picked_twostage_sigmoid_po_kernel(
                     scales[0].bitcast(I32)[4 * q : 4 * q + 4, :],
                 )
 
-        deal_words(d_w, d_w_g)
+        xo_sc = sb("xo_sc", [P, PICKED], U8)
+        nc.vector.tensor_copy(xo_sc[:], x_sc_tab[:].indirect(own_t[:]))
+        d_w = sb("d_w", [P, PICKED], U32)
+        nc.vector.tensor_copy(d_w[:], d_w_tab[:].indirect(kidx_t[:]))
         xq_w = []
         for half in range(2):
-            xq_half = sb(f"xq_w{half}", [P, PICKED // 2], U32, tag=f"query{half}")
+            xq_half = sb(f"xq_w{half}", [P, PICKED // 2], U32)
             nc.vector.tensor_copy(xq_half[:], x_w_tab[:].indirect(offs_t[:, 16 * half : 16 * half + 16]))
             xq_w.append(xq_half)
         xo_w = sb("xo_w", [P, PICKED], U32)
@@ -128,31 +130,31 @@ def tile_picked_twostage_sigmoid_po_kernel(
         def cols(i):
             return slice(i * CHUNK, (i + 1) * CHUNK)
 
-        s_sb = []
+        s_banks = []
         for c in range(CHUNKS):
-            bank = psum.tile([P, PACK, CHUNK], F32, name=f"score{c}", tag=f"a{c}")
+            bank = psum.tile([P, PICKED], F32, name=f"score{c}", tag=f"a{c}")
+            mx(bank[:], xq_w[c // 2][:, cols(c % 2)], xq_sc[:, cols(c)], d_w[:], d_sc[:])
+            s = sb(f"s{c}", [P, PACK, P], F32)
+            nc.scalar.activation(s[:], bank[:].rearrange("j (m t) -> j t m", t=PACK), SIGMOID, scale=0.0625)
+            turned = psum.tile([P, PACK, CHUNK], F32, name=f"turned{c}", tag=f"b{c}")
             for t in range(PACK):
-                mx(bank[:, t, :], d_w[:, cols(t)], d_sc[:, cols(t)], xq_w[c // 2][:, cols(c % 2)], xq_sc[:, cols(c)])
-            s = sb(f"s{c}", [P, CHUNK, PACK], F32)
-            nc.scalar.activation(s[:], bank[:].rearrange("p t n -> p n t"), SIGMOID, scale=0.0625)
-            s_sb.append(s)
+                nc.tensor.transpose(turned[:, t, :], s[:, t, :], identity[:])
+            s_banks.append(turned)
 
-        xo_sc = sb("xo_sc", [P, PICKED], U8, tag="query0")
-        nc.vector.tensor_copy(xo_sc[:], x_sc_tab[:].indirect(own_t[:]))
-        h_banks, y_bf = {}, {}
+        h_banks, y_sb, y_bf = {}, {}, {}
 
         def weigh(c):
             nc.vector.tensor_tensor(
-                z_bf[:, c * PACK * CHUNK : (c + 1) * PACK * CHUNK],
-                s_sb[c][:].rearrange("p n t -> p (n t)"), gain[:].rearrange("p n t -> p (n t)"), MULT,
+                z_bf[:, c * PACK * CHUNK : (c + 1) * PACK * CHUNK].rearrange("p (n t) -> p n t", t=PACK),
+                s_banks[c][:].rearrange("p t n -> p n t"), gain[:], MULT,
             )
 
         deal_bytes(w_sc, w_sc_raw)
-        z_bf = sb("z_bf", [P, PACK * PICKED], BF16, tag="d_table")
+        z_bf = sb("z_bf", [P, PACK * PICKED], BF16, tag="scratch")
         val_sb = {}
 
         def projection(c):
-            bank = psum.tile([P, PACK, CHUNK], F32, name=f"val{c}", tag=f"b{c}")
+            bank = psum.tile([P, PACK, CHUNK], F32, name=f"val{c}", tag=f"a{c}" if c < 2 else f"b{c}")
             for t in range(PACK):
                 mx(bank[:, t, :], w2_w[:, cols(t)], w_sc[4:P, cols(t)], xo_w[:, cols(c)], xo_sc[:, cols(c)])
             v = sb(f"v{c}", [P, PACK, CHUNK], F32)
@@ -167,23 +169,22 @@ def tile_picked_twostage_sigmoid_po_kernel(
             zw = sb(f"zw{c}", [P, CHUNK], U32)
             zs = sb(f"zs{c}", [P, CHUNK], U8)
             nc.vector.quantize_mx(zw[:].bitcast(FP8X4), zs[:], z_bf[:, c * PACK * CHUNK : (c + 1) * PACK * CHUNK])
-            h_banks[c] = psum.tile([P, PACK, CHUNK], F32, name=f"h{c}", tag=f"a{c}")
+            h_banks[c] = psum.tile([P, PACK, CHUNK], F32, name=f"h{c}", tag=f"b{c}" if c < 2 else f"a{c}")
             for t in range(PACK):
                 mx(h_banks[c][:, t, :], w1_w[:, cols(t)], w_sc[:, cols(t)], zw[:], zs[:])
 
         def result(c):
             y = sb(f"y{c}", [P, PACK, CHUNK], F32)
             y_bf[c] = sb(f"yb{c}", [P, CHUNK, PACK], BF16)
-            parts = 2 if c == CHUNKS - 1 else 1
-            width = CHUNK // parts
-            for part in range(parts):
-                n = slice(part * width, (part + 1) * width)
-                nc.vector.tensor_tensor(y[:, :, n], h_banks[c][:, :, n], val_sb[c][:, :, n], MULT)
-                nc.scalar.copy(
-                    y_bf[c][:, n, :].rearrange("p (m i) t -> p m t i", i=4),
-                    y[:, :, n].rearrange("p t (m i) -> p m t i", i=4),
-                )
+            nc.vector.tensor_tensor(y[:], h_banks[c][:], val_sb[c][:], MULT)
             nc.sync.dma_start(out_rows[:, :, cols(c)], y[:])
+            y_sb[c] = y
+
+        def rounded(c, copy):
+            copy(
+                y_bf[c][:].rearrange("p (m i) t -> p m t i", i=4),
+                y_sb[c][:].rearrange("p t (m i) -> p m t i", i=4),
+            )
 
         def planes(c):
             nc.vector.quantize_mx(
@@ -198,19 +199,23 @@ def tile_picked_twostage_sigmoid_po_kernel(
         projection(1)
         weigh(1)
         second_product(0)
-        projection(2)
         weigh(2)
         second_product(1)
-        projection(3)
-        result(0)
+        projection(2)
         weigh(3)
+        result(0)
+        rounded(0, nc.scalar.copy)
         second_product(2)
+        projection(3)
         result(1)
+        rounded(1, nc.scalar.copy)
         second_product(3)
         planes(0)
         result(2)
+        rounded(2, nc.scalar.copy)
         planes(1)
         result(3)
+        rounded(3, nc.vector.tensor_copy)
         planes(2)
         planes(3)
         for q in range(QUADS):

@@ -15,11 +15,15 @@ SIGMOID = mybir.ActivationFunctionType.Sigmoid
 
 P = 128
 PACK = 4
-TABLE = 2048
-PICKED = 512
-CHUNK = 128
-CHUNKS = PICKED // CHUNK
 QUADS = 4
+ROWS = 4
+TABLE = 2048
+WIDTH = 512
+HALF = WIDTH // 2
+CHUNK = 128
+CHUNKS = WIDTH // CHUNK
+LINE = 16
+W1_FIRST, W2_FIRST = 0, 4
 FLOPS = 3 * 2 * 512 * 512 * 512
 
 
@@ -32,194 +36,179 @@ def tile_picked_twostage_sigmoid_po_kernel(
     def words_of(dram):
         return dram[0].rearrange("p n t -> p (n t)").bitcast(I32)
 
-    def deal_words(dst, src):
+    def scale_rows(dram, q):
+        return dram[0].bitcast(I32)[ROWS * q : ROWS * (q + 1), :]
+
+    def scale_partitions(tile, q, first=0):
+        return tile[:].bitcast(I32)[32 * q + first : 32 * q + first + ROWS, :]
+
+    def deal(dst, src, run):
         nc.vector.tensor_copy(
-            out=dst[:].rearrange("p (t c i) -> p c t i", t=PACK, i=4),
-            in_=src[:].rearrange("p (c i t) -> p c t i", t=PACK, i=4),
+            out=dst[:].rearrange("p (t c i) -> p c t i", t=PACK, i=run),
+            in_=src[:].rearrange("p (c i t) -> p c t i", t=PACK, i=run),
         )
 
-    def deal_bytes(dst, src):
-        nc.vector.tensor_copy(
-            out=dst[:].rearrange("p (t c i) -> p c t i", t=PACK, i=16),
-            in_=src[:].rearrange("p (c i t) -> p c t i", t=PACK, i=16),
-        )
+    def gather(dst, table, offsets):
+        nc.vector.tensor_copy(dst[:], table[:].indirect(offsets))
 
-    def mx(out, lhs_words, lhs_scales, rhs_words, rhs_scales):
+    def product(out, lhs_words, lhs_scales, rhs_words, rhs_scales):
         nc.tensor.matmul_mx(
             out=out, lhsT=lhs_words.bitcast(FP8X4), lhsT_scale=lhs_scales,
             rhs=rhs_words.bitcast(FP8X4), rhs_scale=rhs_scales, start=True, stop=True,
         )
 
+    def block(i, width=CHUNK):
+        return slice(i * width, (i + 1) * width)
+
+    def list_half(half):
+        return block(half, HALF // 16)
+
     with ExitStack() as ctx:
         keep = ctx.enter_context(tc.tile_pool(name="keep", bufs=1))
         psum = ctx.enter_context(tc.psum_pool(name="psum", bufs=1))
 
-        def sb(name, shape, dtype, tag=""):
+        def sbuf(name, shape, dtype, tag=""):
             return keep.tile(shape, dtype, name=name, tag=tag, align_bytes=64)
 
-        kidx_t = sb("kidx_t", [P, PICKED // 16], U16)
-        offs_t = sb("offs_t", [P, PICKED // 16], U16)
-        own_t = sb("own_t", [P, PICKED // 16], U16)
-        d_sc_tab = sb("d_sc_tab", [P, TABLE], U8, tag="scratch")
-        x_sc_tab = sb("x_sc_tab", [P, TABLE], U8)
-        d_sc = sb("d_sc", [P, PICKED], U8)
-        gn_t = sb("gn_t", [P, PACK], F32, tag="d_table")
-        w1_raw = sb("w1_raw", [P, PICKED], U32)
-        w2_raw = sb("w2_raw", [P, PICKED], U32, tag="x_table")
+        kidx_list = sbuf("kidx_list", [P, WIDTH // 16], U16)
+        offs_list = sbuf("offs_list", [P, WIDTH // 16], U16)
+        own_list = sbuf("own_list", [P, WIDTH // 16], U16)
+        d_scale_table = sbuf("d_scale_table", [P, TABLE], U8, tag="scratch")
+        x_scale_table = sbuf("x_scale_table", [P, TABLE], U8)
+        key_scales = sbuf("key_scales", [P, WIDTH], U8)
+        gn_raw = sbuf("gn_raw", [P, PACK], F32, tag="d_table")
+        w1_raw = sbuf("w1_raw", [P, WIDTH], U32)
+        w2_raw = sbuf("w2_raw", [P, WIDTH], U32, tag="x_table")
 
-        nc.vector.memset(d_sc_tab[:].bitcast(I32), 0)
-        nc.vector.memset(x_sc_tab[:].bitcast(I32), 0)
-        nc.vector.memset(d_sc[:].bitcast(I32), 0)
+        nc.vector.memset(d_scale_table[:].bitcast(I32), 0)
+        nc.vector.memset(x_scale_table[:].bitcast(I32), 0)
+        nc.vector.memset(key_scales[:].bitcast(I32), 0)
 
-        identity = sb("identity", [P, P], F32)
+        identity = sbuf("identity", [P, P], F32)
         make_identity(nc, identity[:])
 
-        nc.sync.dma_start(gn_t[:], gn.rearrange("(p t) o -> p (t o)", t=PACK))
-        nc.sync.dma_start(kidx_t[:], kidx)
-        nc.sync.dma_start(offs_t[:], offs)
-        nc.sync.dma_start(own_t[:], own)
+        nc.sync.dma_start(gn_raw[:], gn.rearrange("(p t) o -> p (t o)", t=PACK))
+        nc.sync.dma_start(kidx_list[:], kidx)
+        nc.sync.dma_start(offs_list[:], offs)
+        nc.sync.dma_start(own_list[:], own)
         nc.sync.dma_start(w2_raw[:].bitcast(I32), words_of(w2_words))
         nc.sync.dma_start(w1_raw[:].bitcast(I32), words_of(w1_words))
-        nc.sync.dma_start(d_sc_tab[:].bitcast(I32)[0:P:8, :], d_scales[0].bitcast(I32))
+        nc.sync.dma_start(d_scale_table[:].bitcast(I32)[0:P:8, :], d_scales[0].bitcast(I32))
+        for q in range(QUADS):
+            nc.sync.dma_start(scale_partitions(x_scale_table, q), scale_rows(x_scales, q))
+
+        gain = sbuf("gain", [P, CHUNK, PACK], F32)
+        nc.vector.tensor_copy(gain[:], gn_raw[:].unsqueeze(1).to_broadcast([P, CHUNK, PACK]))
+        d_word_table = sbuf("d_word_table", [P, TABLE], U32, tag="d_table")
+        nc.sync.dma_start(d_word_table[:].bitcast(I32), words_of(d_words))
+        w2_dealt = sbuf("w2_dealt", [P, WIDTH], U32)
+        w1_dealt = sbuf("w1_dealt", [P, WIDTH], U32)
+        deal(w2_dealt, w2_raw, LINE // 4)
+        x_word_table = sbuf("x_word_table", [P, TABLE], U32, tag="x_table")
+        nc.sync.dma_start(x_word_table[:].bitcast(I32), words_of(x_words))
+        deal(w1_dealt, w1_raw, LINE // 4)
+
+        picked_scales = sbuf("picked_scales", [P, WIDTH], U8)
+        gather(picked_scales, d_scale_table, kidx_list[:])
         for q in range(QUADS):
             nc.sync.dma_start(
-                x_sc_tab[:].bitcast(I32)[32 * q : 32 * q + 4, :], x_scales[0].bitcast(I32)[4 * q : 4 * q + 4, :]
+                scale_partitions(key_scales, q), picked_scales[:].bitcast(I32)[32 * q : 32 * (q + 1) : 8, :]
             )
-        gain = sb("gain", [P, CHUNK, PACK], F32)
-        nc.vector.tensor_copy(gain[:], gn_t[:].unsqueeze(1).to_broadcast([P, CHUNK, PACK]))
-        d_w_tab = sb("d_w_tab", [P, TABLE], U32, tag="d_table")
-        nc.sync.dma_start(d_w_tab[:].bitcast(I32), words_of(d_words))
+        query_scales = sbuf("query_scales", [P, WIDTH], U8)
+        gather(query_scales, x_scale_table, offs_list[:])
 
-        w2_w = sb("w2_w", [P, PICKED], U32)
-        w1_w = sb("w1_w", [P, PICKED], U32)
-        deal_words(w2_w, w2_raw)
-        x_w_tab = sb("x_w_tab", [P, TABLE], U32, tag="x_table")
-        nc.sync.dma_start(x_w_tab[:].bitcast(I32), words_of(x_words))
-        deal_words(w1_w, w1_raw)
-        d_sc_g = sb("d_sc_g", [P, PICKED], U8)
-        nc.vector.tensor_copy(d_sc_g[:], d_sc_tab[:].indirect(kidx_t[:]))
-        for q in range(QUADS):
-            nc.sync.dma_start(
-                d_sc[:].bitcast(I32)[32 * q : 32 * q + 4, :], d_sc_g[:].bitcast(I32)[32 * q : 32 * q + 32 : 8, :]
-            )
-
-        xq_sc = sb("xq_sc", [P, PICKED], U8)
-        nc.vector.tensor_copy(xq_sc[:], x_sc_tab[:].indirect(offs_t[:]))
-        w_sc_raw = sb("w_sc_raw", [P, PICKED], U8, tag="scratch")
-        nc.vector.memset(w_sc_raw[:].bitcast(I32), 0)
-        for first, scales in ((4, w2_scales), (0, w1_scales)):
+        w_scales_raw = sbuf("w_scales_raw", [P, WIDTH], U8, tag="scratch")
+        nc.vector.memset(w_scales_raw[:].bitcast(I32), 0)
+        for first, scales in ((W2_FIRST, w2_scales), (W1_FIRST, w1_scales)):
             for q in range(QUADS):
-                nc.sync.dma_start(
-                    w_sc_raw[:].bitcast(I32)[32 * q + first : 32 * q + first + 4, :],
-                    scales[0].bitcast(I32)[4 * q : 4 * q + 4, :],
-                )
+                nc.sync.dma_start(scale_partitions(w_scales_raw, q, first), scale_rows(scales, q))
 
-        xo_sc = sb("xo_sc", [P, PICKED], U8)
-        nc.vector.tensor_copy(xo_sc[:], x_sc_tab[:].indirect(own_t[:]))
-        d_w = sb("d_w", [P, PICKED], U32)
-        nc.vector.tensor_copy(d_w[:], d_w_tab[:].indirect(kidx_t[:]))
-        xq_w = []
+        own_scales = [sbuf("own_scales0", [P, HALF], U8)]
+        gather(own_scales[0], x_scale_table, own_list[:, list_half(0)])
+        key_words = sbuf("key_words", [P, WIDTH], U32)
+        gather(key_words, d_word_table, kidx_list[:])
+        query_words = []
         for half in range(2):
-            xq_half = sb(f"xq_w{half}", [P, PICKED // 2], U32)
-            nc.vector.tensor_copy(xq_half[:], x_w_tab[:].indirect(offs_t[:, 16 * half : 16 * half + 16]))
-            xq_w.append(xq_half)
-        xo_w = sb("xo_w", [P, PICKED], U32)
-        nc.vector.tensor_copy(xo_w[:], x_w_tab[:].indirect(own_t[:]))
-        w_sc = sb("w_sc", [P, PICKED], U8, tag="x_table")
+            query_words.append(sbuf(f"query_words{half}", [P, HALF], U32, tag=f"query{half}"))
+            gather(query_words[half], x_word_table, offs_list[:, list_half(half)])
+        own_words = sbuf("own_words", [P, WIDTH], U32)
+        gather(own_words, x_word_table, own_list[:])
 
-        def cols(i):
-            return slice(i * CHUNK, (i + 1) * CHUNK)
-
-        s_banks = []
+        sigmoids = []
         for c in range(CHUNKS):
-            bank = psum.tile([P, PICKED], F32, name=f"score{c}", tag=f"a{c}")
-            mx(bank[:], xq_w[c // 2][:, cols(c % 2)], xq_sc[:, cols(c)], d_w[:], d_sc[:])
-            s = sb(f"s{c}", [P, PACK, P], F32)
-            nc.scalar.activation(s[:], bank[:].rearrange("j (m t) -> j t m", t=PACK), SIGMOID, scale=0.0625)
-            turned = psum.tile([P, PACK, CHUNK], F32, name=f"turned{c}", tag=f"b{c}")
+            scores = psum.tile([CHUNK, WIDTH], F32, name=f"scores{c}", tag=f"first{c}")
+            product(
+                scores[:], query_words[c // 2][:, block(c % 2)], query_scales[:, block(c)], key_words[:], key_scales[:]
+            )
+            by_query = sbuf(f"by_query{c}", [CHUNK, PACK, P], F32)
+            nc.scalar.activation(by_query[:], scores[:].rearrange("n (p t) -> n t p", t=PACK), SIGMOID, scale=0.0625)
+            by_key = psum.tile([P, PACK, CHUNK], F32, name=f"by_key{c}", tag=f"second{c}")
             for t in range(PACK):
-                nc.tensor.transpose(turned[:, t, :], s[:, t, :], identity[:])
-            s_banks.append(turned)
+                nc.tensor.transpose(by_key[:, t, :], by_query[:, t, :], identity[:])
+            sigmoids.append(by_key)
 
-        h_banks, y_sb, y_bf = {}, {}, {}
+        own_scales.append(sbuf("own_scales1", [P, HALF], U8, tag="query0"))
+        gather(own_scales[1], x_scale_table, own_list[:, list_half(1)])
+        w_scales = sbuf("w_scales", [P, WIDTH], U8, tag="x_table")
+        deal(w_scales, w_scales_raw, LINE)
+        z = sbuf("z", [P, CHUNKS, CHUNK * PACK], BF16, tag="scratch")
+        y_words = sbuf("y_words", [P, WIDTH], U32)
+        y_scales = sbuf("y_scales", [P, WIDTH], U8)
+        out_rows = out_0.rearrange("(p t) n -> p t n", t=PACK)
+        val, h, y_rounded = {}, {}, {}
 
         def weigh(c):
             nc.vector.tensor_tensor(
-                z_bf[:, c * PACK * CHUNK : (c + 1) * PACK * CHUNK].rearrange("p (n t) -> p n t", t=PACK),
-                s_banks[c][:].rearrange("p t n -> p n t"), gain[:], MULT,
+                z[:, c, :].rearrange("p (n t) -> p n t", t=PACK), sigmoids[c][:].rearrange("p t n -> p n t"),
+                gain[:], MULT,
             )
 
-        deal_bytes(w_sc, w_sc_raw)
-        z_bf = sb("z_bf", [P, PACK * PICKED], BF16, tag="scratch")
-        val_sb = {}
+        def is_early(c):
+            return c < CHUNKS // 2
 
-        def projection(c):
-            bank = psum.tile([P, PACK, CHUNK], F32, name=f"val{c}", tag=f"a{c}" if c < 2 else f"b{c}")
+        def project(c):
+            bank = psum.tile([P, PACK, CHUNK], F32, name=f"val{c}", tag=f"first{c}" if is_early(c) else f"second{c}")
             for t in range(PACK):
-                mx(bank[:, t, :], w2_w[:, cols(t)], w_sc[4:P, cols(t)], xo_w[:, cols(c)], xo_sc[:, cols(c)])
-            v = sb(f"v{c}", [P, PACK, CHUNK], F32)
-            nc.scalar.copy(v[:], bank[:])
-            val_sb[c] = v
+                product(
+                    bank[:, t, :], w2_dealt[:, block(t)], w_scales[W2_FIRST:P, block(t)],
+                    own_words[:, block(c)], own_scales[c // 2][:, block(c % 2)],
+                )
+            val[c] = sbuf(f"val_sbuf{c}", [P, PACK, CHUNK], F32)
+            nc.scalar.copy(val[c][:], bank[:])
 
-        y_w = sb("y_w", [P, PICKED], U32)
-        y_sc = sb("y_sc", [P, PICKED], U8)
-        out_rows = out_0.rearrange("(p t) j -> p t j", t=PACK)
-
-        def second_product(c):
-            zw = sb(f"zw{c}", [P, CHUNK], U32)
-            zs = sb(f"zs{c}", [P, CHUNK], U8)
-            nc.vector.quantize_mx(zw[:].bitcast(FP8X4), zs[:], z_bf[:, c * PACK * CHUNK : (c + 1) * PACK * CHUNK])
-            h_banks[c] = psum.tile([P, PACK, CHUNK], F32, name=f"h{c}", tag=f"b{c}" if c < 2 else f"a{c}")
+        def read_values(c):
+            z_words = sbuf(f"z_words{c}", [P, CHUNK], U32)
+            z_scales = sbuf(f"z_scales{c}", [P, CHUNK], U8)
+            nc.vector.quantize_mx(z_words[:].bitcast(FP8X4), z_scales[:], z[:, c, :])
+            h[c] = psum.tile([P, PACK, CHUNK], F32, name=f"h{c}", tag=f"second{c}" if is_early(c) else f"first{c}")
             for t in range(PACK):
-                mx(h_banks[c][:, t, :], w1_w[:, cols(t)], w_sc[:, cols(t)], zw[:], zs[:])
+                product(h[c][:, t, :], w1_dealt[:, block(t)], w_scales[W1_FIRST:P, block(t)], z_words[:], z_scales[:])
 
-        def result(c):
-            y = sb(f"y{c}", [P, PACK, CHUNK], F32)
-            y_bf[c] = sb(f"yb{c}", [P, CHUNK, PACK], BF16)
-            nc.vector.tensor_tensor(y[:], h_banks[c][:], val_sb[c][:], MULT)
-            nc.sync.dma_start(out_rows[:, :, cols(c)], y[:])
-            y_sb[c] = y
-
-        def rounded(c, copy):
+        def combine(c):
+            y = sbuf(f"y{c}", [P, PACK, CHUNK], F32)
+            nc.vector.tensor_tensor(y[:], h[c][:], val[c][:], MULT)
+            nc.sync.dma_start(out_rows[:, :, block(c)], y[:])
+            y_rounded[c] = sbuf(f"y_rounded{c}", [P, CHUNK, PACK], BF16)
+            copy = nc.vector.tensor_copy if c == CHUNKS - 1 else nc.scalar.copy
             copy(
-                y_bf[c][:].rearrange("p (m i) t -> p m t i", i=4),
-                y_sb[c][:].rearrange("p t (m i) -> p m t i", i=4),
+                y_rounded[c][:].rearrange("p (m i) t -> p m t i", i=LINE // 4),
+                y[:].rearrange("p t (m i) -> p m t i", i=LINE // 4),
             )
 
-        def planes(c):
+        def quantise_result(c):
             nc.vector.quantize_mx(
-                y_w[:, cols(c)].bitcast(FP8X4), y_sc[:, cols(c)], y_bf[c][:].rearrange("p n t -> p (n t)")
+                y_words[:, block(c)].bitcast(FP8X4), y_scales[:, block(c)], y_rounded[c][:].rearrange("p n t -> p (n t)")
             )
             if c % 2:
-                pair = slice((c - 1) * CHUNK, (c + 1) * CHUNK)
-                nc.sync.dma_start(words_of(out_1)[:, pair], y_w[:].bitcast(I32)[:, pair])
+                pair = block(c // 2, 2 * CHUNK)
+                nc.sync.dma_start(words_of(out_1)[:, pair], y_words[:].bitcast(I32)[:, pair])
 
-        projection(0)
-        weigh(0)
-        projection(1)
-        weigh(1)
-        second_product(0)
-        weigh(2)
-        second_product(1)
-        projection(2)
-        weigh(3)
-        result(0)
-        rounded(0, nc.scalar.copy)
-        second_product(2)
-        projection(3)
-        result(1)
-        rounded(1, nc.scalar.copy)
-        second_product(3)
-        planes(0)
-        result(2)
-        rounded(2, nc.scalar.copy)
-        planes(1)
-        result(3)
-        rounded(3, nc.vector.tensor_copy)
-        planes(2)
-        planes(3)
+        stages = ((weigh, 0), (combine, 3), (read_values, 1), (project, 0), (quantise_result, 4))
+        for step in range(CHUNKS + 4):
+            for stage, lag in stages:
+                if 0 <= step - lag < CHUNKS:
+                    stage(step - lag)
+
         for q in range(QUADS):
             queue = nc.sync if q == QUADS - 1 else nc.scalar
-            queue.dma_start(
-                out_2[0].bitcast(I32)[4 * q : 4 * q + 4, :], y_sc[:].bitcast(I32)[32 * q : 32 * q + 4, :]
-            )
+            queue.dma_start(scale_rows(out_2, q), scale_partitions(y_scales, q))

from contextlib import ExitStack

import concourse.mybir as mybir
from concourse.masks import make_identity

F32 = mybir.dt.float32
BF16 = mybir.dt.bfloat16
I32 = mybir.dt.int32
U32 = mybir.dt.uint32
U16 = mybir.dt.uint16
U8 = mybir.dt.uint8
FP8X4 = mybir.dt.float8_e4m3fn_x4
MULT = mybir.AluOpType.mult
SIGMOID = mybir.ActivationFunctionType.Sigmoid

P = 128
PACK = 4
QUADS = 4
ROWS = 4
TABLE = 2048
WIDTH = 512
HALF = WIDTH // 2
CHUNK = 128
CHUNKS = WIDTH // CHUNK
LINE = 16
W1_FIRST, W2_FIRST = 0, 4
FLOPS = 3 * 2 * 512 * 512 * 512


def tile_picked_twostage_sigmoid_po_kernel(
    tc, x_words, x_scales, d_words, d_scales, gn, w1_words, w1_scales, w2_words, w2_scales, offs, kidx, own,
    out_0, out_1, out_2,
):
    nc = tc.nc

    def words_of(dram):
        return dram[0].rearrange("p n t -> p (n t)").bitcast(I32)

    def scale_rows(dram, q):
        return dram[0].bitcast(I32)[ROWS * q : ROWS * (q + 1), :]

    def scale_partitions(tile, q, first=0):
        return tile[:].bitcast(I32)[32 * q + first : 32 * q + first + ROWS, :]

    def deal(dst, src, run):
        nc.vector.tensor_copy(
            out=dst[:].rearrange("p (t c i) -> p c t i", t=PACK, i=run),
            in_=src[:].rearrange("p (c i t) -> p c t i", t=PACK, i=run),
        )

    def gather(dst, table, offsets):
        nc.vector.tensor_copy(dst[:], table[:].indirect(offsets))

    def product(out, lhs_words, lhs_scales, rhs_words, rhs_scales):
        nc.tensor.matmul_mx(
            out=out, lhsT=lhs_words.bitcast(FP8X4), lhsT_scale=lhs_scales,
            rhs=rhs_words.bitcast(FP8X4), rhs_scale=rhs_scales, start=True, stop=True,
        )

    def block(i, width=CHUNK):
        return slice(i * width, (i + 1) * width)

    def list_half(half):
        return block(half, HALF // 16)

    with ExitStack() as ctx:
        keep = ctx.enter_context(tc.tile_pool(name="keep", bufs=1))
        psum = ctx.enter_context(tc.psum_pool(name="psum", bufs=1))

        def sbuf(name, shape, dtype, tag=""):
            return keep.tile(shape, dtype, name=name, tag=tag, align_bytes=64)

        kidx_list = sbuf("kidx_list", [P, WIDTH // 16], U16)
        offs_list = sbuf("offs_list", [P, WIDTH // 16], U16)
        own_list = sbuf("own_list", [P, WIDTH // 16], U16)
        d_scale_table = sbuf("d_scale_table", [P, TABLE], U8, tag="scratch")
        x_scale_table = sbuf("x_scale_table", [P, TABLE], U8)
        key_scales = sbuf("key_scales", [P, WIDTH], U8)
        gn_raw = sbuf("gn_raw", [P, PACK], F32, tag="d_table")
        w1_raw = sbuf("w1_raw", [P, WIDTH], U32)
        w2_raw = sbuf("w2_raw", [P, WIDTH], U32, tag="x_table")

        nc.vector.memset(d_scale_table[:].bitcast(I32), 0)
        nc.vector.memset(x_scale_table[:].bitcast(I32), 0)
        nc.vector.memset(key_scales[:].bitcast(I32), 0)

        identity = sbuf("identity", [P, P], F32)
        make_identity(nc, identity[:])

        nc.sync.dma_start(gn_raw[:], gn.rearrange("(p t) o -> p (t o)", t=PACK))
        nc.sync.dma_start(kidx_list[:], kidx)
        nc.sync.dma_start(offs_list[:], offs)
        nc.sync.dma_start(own_list[:], own)
        nc.sync.dma_start(w2_raw[:].bitcast(I32), words_of(w2_words))
        nc.sync.dma_start(w1_raw[:].bitcast(I32), words_of(w1_words))
        nc.sync.dma_start(d_scale_table[:].bitcast(I32)[0:P:8, :], d_scales[0].bitcast(I32))
        for q in range(QUADS):
            nc.sync.dma_start(scale_partitions(x_scale_table, q), scale_rows(x_scales, q))

        gain = sbuf("gain", [P, CHUNK, PACK], F32)
        nc.vector.tensor_copy(gain[:], gn_raw[:].unsqueeze(1).to_broadcast([P, CHUNK, PACK]))
        d_word_table = sbuf("d_word_table", [P, TABLE], U32, tag="d_table")
        nc.sync.dma_start(d_word_table[:].bitcast(I32), words_of(d_words))
        w2_dealt = sbuf("w2_dealt", [P, WIDTH], U32)
        w1_dealt = sbuf("w1_dealt", [P, WIDTH], U32)
        deal(w2_dealt, w2_raw, LINE // 4)
        x_word_table = sbuf("x_word_table", [P, TABLE], U32, tag="x_table")
        nc.sync.dma_start(x_word_table[:].bitcast(I32), words_of(x_words))
        deal(w1_dealt, w1_raw, LINE // 4)

        picked_scales = sbuf("picked_scales", [P, WIDTH], U8)
        gather(picked_scales, d_scale_table, kidx_list[:])
        for q in range(QUADS):
            nc.sync.dma_start(
                scale_partitions(key_scales, q), picked_scales[:].bitcast(I32)[32 * q : 32 * (q + 1) : 8, :]
            )
        query_scales = sbuf("query_scales", [P, WIDTH], U8)
        gather(query_scales, x_scale_table, offs_list[:])

        w_scales_raw = sbuf("w_scales_raw", [P, WIDTH], U8, tag="scratch")
        nc.vector.memset(w_scales_raw[:].bitcast(I32), 0)
        for first, scales in ((W2_FIRST, w2_scales), (W1_FIRST, w1_scales)):
            for q in range(QUADS):
                nc.sync.dma_start(scale_partitions(w_scales_raw, q, first), scale_rows(scales, q))

        own_scales = [sbuf("own_scales0", [P, HALF], U8)]
        gather(own_scales[0], x_scale_table, own_list[:, list_half(0)])
        key_words = sbuf("key_words", [P, WIDTH], U32)
        gather(key_words, d_word_table, kidx_list[:])
        query_words = []
        for half in range(2):
            query_words.append(sbuf(f"query_words{half}", [P, HALF], U32, tag=f"query{half}"))
            gather(query_words[half], x_word_table, offs_list[:, list_half(half)])
        own_words = sbuf("own_words", [P, WIDTH], U32)
        gather(own_words, x_word_table, own_list[:])

        sigmoids = []
        for c in range(CHUNKS):
            scores = psum.tile([CHUNK, WIDTH], F32, name=f"scores{c}", tag=f"first{c}")
            product(
                scores[:], query_words[c // 2][:, block(c % 2)], query_scales[:, block(c)], key_words[:], key_scales[:]
            )
            by_query = sbuf(f"by_query{c}", [CHUNK, PACK, P], F32)
            nc.scalar.activation(by_query[:], scores[:].rearrange("n (p t) -> n t p", t=PACK), SIGMOID, scale=0.0625)
            by_key = psum.tile([P, PACK, CHUNK], F32, name=f"by_key{c}", tag=f"second{c}")
            for t in range(PACK):
                nc.tensor.transpose(by_key[:, t, :], by_query[:, t, :], identity[:])
            sigmoids.append(by_key)

        own_scales.append(sbuf("own_scales1", [P, HALF], U8, tag="query0"))
        gather(own_scales[1], x_scale_table, own_list[:, list_half(1)])
        w_scales = sbuf("w_scales", [P, WIDTH], U8, tag="x_table")
        deal(w_scales, w_scales_raw, LINE)
        z = sbuf("z", [P, CHUNKS, CHUNK * PACK], BF16, tag="scratch")
        y_words = sbuf("y_words", [P, WIDTH], U32)
        y_scales = sbuf("y_scales", [P, WIDTH], U8)
        out_rows = out_0.rearrange("(p t) n -> p t n", t=PACK)
        val, h, y_rounded = {}, {}, {}

        def weigh(c):
            nc.vector.tensor_tensor(
                z[:, c, :].rearrange("p (n t) -> p n t", t=PACK), sigmoids[c][:].rearrange("p t n -> p n t"),
                gain[:], MULT,
            )

        def is_early(c):
            return c < CHUNKS // 2

        def project(c):
            bank = psum.tile([P, PACK, CHUNK], F32, name=f"val{c}", tag=f"first{c}" if is_early(c) else f"second{c}")
            for t in range(PACK):
                product(
                    bank[:, t, :], w2_dealt[:, block(t)], w_scales[W2_FIRST:P, block(t)],
                    own_words[:, block(c)], own_scales[c // 2][:, block(c % 2)],
                )
            val[c] = sbuf(f"val_sbuf{c}", [P, PACK, CHUNK], F32)
            nc.scalar.copy(val[c][:], bank[:])

        def read_values(c):
            z_words = sbuf(f"z_words{c}", [P, CHUNK], U32)
            z_scales = sbuf(f"z_scales{c}", [P, CHUNK], U8)
            nc.vector.quantize_mx(z_words[:].bitcast(FP8X4), z_scales[:], z[:, c, :])
            h[c] = psum.tile([P, PACK, CHUNK], F32, name=f"h{c}", tag=f"second{c}" if is_early(c) else f"first{c}")
            for t in range(PACK):
                product(h[c][:, t, :], w1_dealt[:, block(t)], w_scales[W1_FIRST:P, block(t)], z_words[:], z_scales[:])

        def combine(c):
            y = sbuf(f"y{c}", [P, PACK, CHUNK], F32)
            nc.vector.tensor_tensor(y[:], h[c][:], val[c][:], MULT)
            nc.sync.dma_start(out_rows[:, :, block(c)], y[:])
            y_rounded[c] = sbuf(f"y_rounded{c}", [P, CHUNK, PACK], BF16)
            copy = nc.vector.tensor_copy if c == CHUNKS - 1 else nc.scalar.copy
            copy(
                y_rounded[c][:].rearrange("p (m i) t -> p m t i", i=LINE // 4),
                y[:].rearrange("p t (m i) -> p m t i", i=LINE // 4),
            )

        def quantise_result(c):
            nc.vector.quantize_mx(
                y_words[:, block(c)].bitcast(FP8X4), y_scales[:, block(c)], y_rounded[c][:].rearrange("p n t -> p (n t)")
            )
            if c % 2:
                pair = block(c // 2, 2 * CHUNK)
                nc.sync.dma_start(words_of(out_1)[:, pair], y_words[:].bitcast(I32)[:, pair])

        stages = ((weigh, 0), (combine, 3), (read_values, 1), (project, 0), (quantise_result, 4))
        for step in range(CHUNKS + 4):
            for stage, lag in stages:
                if 0 <= step - lag < CHUNKS:
                    stage(step - lag)

        for q in range(QUADS):
            queue = nc.sync if q == QUADS - 1 else nc.scalar
            queue.dma_start(scale_rows(out_2, q), scale_partitions(y_scales, q))
